import numpy as np
import ml_dtypes


def mxq(x, axis, fmt="e4m3"):
    dtype, down = {"e4m3": (ml_dtypes.float8_e4m3fn, 7), "e5m2": (ml_dtypes.float8_e5m2, 14)}[fmt]
    v = np.moveaxis(np.asarray(x, np.float32).astype(ml_dtypes.bfloat16).astype(np.float64), axis, -1)
    blocks = v.reshape(v.shape[:-1] + (-1, 32))
    amax = np.abs(blocks).max(-1, keepdims=True)
    byte = np.maximum(np.where(amax > 0, np.frexp(amax)[1] - 1 + 127, 0) - down, 1)
    scale = np.exp2(byte - 127.0)
    codes = (blocks / scale).astype(np.float32).astype(dtype).astype(np.float64)
    return np.moveaxis((codes * scale).reshape(v.shape), -1, axis)


WIDE = False


def mx_kscale(k, group=512):
    if not WIDE:
        return np.ones(k)
    levels = np.array([10, -10, 5, -5, 0])
    if group != 512:
        return np.exp2(np.random.permutation(np.resize(levels, k // group))).repeat(group)
    if k % 512:
        return np.exp2(np.random.permutation(np.resize(levels, k // 32))).repeat(32)
    a = np.empty((k // 512, 16))
    for p in range(k // 512):
        a[p, :8] = np.random.permutation(np.resize(levels, 8))
        for g in range(8):
            far = levels[np.abs(levels - a[p, g]) >= 10]
            a[p, g + 8] = far[np.random.randint(len(far))]
    return np.exp2(a.ravel()).repeat(32)


def f64(x):
    return np.asarray(x).astype(np.float64)


def striped(idx):
    return np.tile(np.asarray(idx).reshape(-1, 16).T, (8, 1)).astype(np.uint16)


def unstriped(offs):
    return offs[:16].T.reshape(-1).astype(np.int64)


H, KV, D, NQ, N = 2, 2, 256, 512, 1024
CAP = 2.0


def setup_inputs():
    n = np.random.standard_normal
    s = mx_kscale(D, 0)[:, None]
    u = mx_kscale(N)
    t = np.random.uniform(0.5, 2.0, N) * u
    v = n((KV, N, 128))
    v[:, :, 127] = 1.0
    return {
        "qT": (n((H, D, NQ)) * s * (0.70 / np.sqrt(D))).astype(np.float32),
        "kT": (n((KV, D, N)) / s).astype(np.float32),
        "t": t.reshape(N, 1).astype(np.float32),
        "v": (v / t[:, None]).astype(np.float32),
    }


def reference(qT, kT, t, v):
    a = mxq(f64(kT), 1, "e4m3").transpose(0, 2, 1) @ mxq(f64(qT), 1, "e4m3")
    a = CAP * np.tanh(a / CAP)
    p = np.square(np.maximum(a, 0.0))
    w = p * f64(t)
    y = mxq(w, 1, "e4m3").transpose(0, 2, 1) @ mxq(f64(v), 1, "e4m3")
    y = y / (y[:, :, 127:128] + 1.0)
    return y

@@ -1,0 +1,230 @@
+from contextlib import ExitStack
+
+import concourse.mybir as mybir
+
+H, D, NQ, N, E = 2, 256, 512, 1024, 128
+FLOPS = 2 * H * N * NQ * D + 2 * H * NQ * N * E
+
+F32 = mybir.dt.float32
+BF16 = mybir.dt.bfloat16
+U32 = mybir.dt.uint32
+U8 = mybir.dt.uint8
+FP8X4 = mybir.dt.float8_e4m3fn_x4
+ACT = mybir.ActivationFunctionType
+ALU = mybir.AluOpType
+
+P = 128
+PACK = 4
+ROWS = D // PACK
+PASS = P * PACK
+PASSES = N // PASS
+QB = 128
+CAP = 2.0
+
+
+def tile_rows_a_relu2_cap_kernel(tc, qT, kT, t, v, out):
+    nc = tc.nc
+    q_rows = qT.rearrange("h (p j) q -> (h p) j q", j=PACK)
+    k_rows = kT.rearrange("h (p j) n -> (h p) j n", j=PACK)
+    v_rows = v.rearrange("h (c p j) e -> c p h (j e)", p=P, j=PACK)
+    t_rows = t.rearrange("(c p j) o -> p c (j o)", p=P, j=PACK)
+    out_rows = out.rearrange("h (b m) e -> b m h e", m=QB)
+
+    with ExitStack() as ctx:
+        sb = ctx.enter_context(tc.tile_pool(name="sb", bufs=1))
+        ps = ctx.enter_context(tc.psum_pool(name="ps", bufs=1))
+        ctx.enter_context(tc.manual_schedule())
+
+        def new(name, shape, dtype):
+            return sb.tile(shape, dtype, name=name, align_bytes=64)
+
+        score_banks = [[ps.tile([P, PACK, QB], F32, name="score_%d_%d" % (h, i)) for i in range(2)] for h in range(H)]
+        y_banks = [ps.tile([P, H, E], F32, name="y_%d" % i) for i in range(4)]
+
+        t_raw = new("t_raw", [P, PASSES, PACK], F32)
+        nc.scalar.dma_start(out=t_raw[:], in_=t_rows)
+
+        def load(name, src, shape):
+            raw = new(name, shape, F32)
+            nc.sync.dma_start(out=raw[:], in_=src)
+            return raw
+
+        half = PASS // 2
+        k0_raw = [load("k0_raw_%d" % i, k_rows[:, :, i * half : (i + 1) * half], [P, PACK, half]) for i in range(2)]
+        q_spans = [(0, 128), (128, 256), (256, 512)]
+        q_raw = [load("q_raw_%d" % a, q_rows[:, :, a:b], [P, PACK, b - a]) for a, b in q_spans]
+        k1_raw = load("k1_raw", k_rows[:, :, PASS:], [P, PACK, PASS])
+        v_raw = [load("v_raw_%d" % c, v_rows[c], [P, H, PACK * E]) for c in range(PASSES)]
+
+        def quantize(codes, scales, src):
+            nc.vector.quantize_mx(out=codes.bitcast(FP8X4), scales=scales, in_=src)
+
+        k_bf = [new("k_bf_%d" % c, [P, PACK, P, PACK], BF16) for c in range(PASSES)]
+        k_codes = [new("k_codes_%d" % c, [P, PASS], U32) for c in range(PASSES)]
+        k_scales = [new("k_scales_%d" % c, [P, PASS], U8) for c in range(PASSES)]
+
+        def k_round(copy, c, i, raw):
+            copy(
+                out=k_bf[c][:, :, i * 64 : (i + 1) * 64, :].rearrange("p r s j -> p s j r"),
+                in_=raw.rearrange("p j (s r) -> p s j r", r=PACK),
+            )
+
+        def k_quantize_half(c, i):
+            for r in range(PACK):
+                cols = slice(r * P + i * 64, r * P + (i + 1) * 64)
+                quantize(k_codes[c][:, cols], k_scales[c][:, cols],
+                         k_bf[c][:, r, i * 64 : (i + 1) * 64, :].rearrange("p s j -> p (s j)"))
+
+        q_bf = [new("q_bf_%d" % a, [P, b - a, PACK], BF16) for a, b in q_spans]
+        q_codes = [new("q_codes_%d" % a, [P, b - a], U32) for a, b in q_spans]
+        q_scales = [new("q_scales_%d" % a, [P, b - a], U8) for a, b in q_spans]
+
+        def q_round(n):
+            nc.vector.tensor_copy(
+                out=q_bf[n][:].rearrange("p (c i) j -> p c j i", i=4),
+                in_=q_raw[n][:].rearrange("p j (c i) -> p c j i", i=4),
+            )
+
+        def q_quantize(n):
+            quantize(q_codes[n][:], q_scales[n][:], q_bf[n][:].rearrange("p q j -> p (q j)"))
+
+        v_bf = [new("v_bf_%d" % c, [P, H, E, PACK], BF16) for c in range(PASSES)]
+        v_codes = [new("v_codes_%d" % c, [P, H * E], U32) for c in range(PASSES)]
+        v_scales = [new("v_scales_%d" % c, [P, H * E], U8) for c in range(PASSES)]
+
+        def v_round(c):
+            nc.scalar.copy(
+                out=v_bf[c][:].rearrange("p h (c i) j -> p h c j i", i=4),
+                in_=v_raw[c][:].rearrange("p h (j c i) -> p h c j i", j=PACK, i=4),
+            )
+
+        def v_quantize(c):
+            quantize(v_codes[c][:], v_scales[c][:], v_bf[c][:].rearrange("p h e j -> p (h e j)"))
+
+        t4 = new("t4", [P, PASSES, PACK], F32)
+
+        units = [(0, 0, (0,)), (0, 0, (1,)), (0, 1, (0, 1)), (0, 2, (0, 1)), (0, 3, (0, 1)),
+                 (1, 0, (0, 1)), (1, 1, (0, 1)), (1, 2, (0, 1)), (1, 3, (0,)), (1, 3, (1,))]
+        th, rt, w_bf, w_codes, w_scales = {}, {}, {}, {}, {}
+        w_of = {}
+        turn = [0, 0]
+
+        def scores(u):
+            c, b, heads = units[u]
+            n = min(b, 2)
+            q_cols = slice(b * QB - q_spans[n][0], (b + 1) * QB - q_spans[n][0])
+            th[u] = new("th_%d" % u, [P, PACK, len(heads) * QB], F32)
+            for x, h in enumerate(heads):
+                bank = score_banks[h][turn[h] % 2]
+                turn[h] = turn[h] + 1
+                rows = slice(h * ROWS, (h + 1) * ROWS)
+                for r in range(PACK):
+                    cols = slice(r * P, (r + 1) * P)
+                    nc.tensor.matmul_mx(
+                        out=bank[:, r, :],
+                        lhsT=k_codes[c][rows, cols].bitcast(FP8X4), lhsT_scale=k_scales[c][rows, cols],
+                        rhs=q_codes[n][rows, q_cols].bitcast(FP8X4), rhs_scale=q_scales[n][rows, q_cols],
+                        start=True, stop=True,
+                    )
+                nc.scalar.activation(out=th[u][:, :, x * QB : (x + 1) * QB], in_=bank[:], func=ACT.Tanh, scale=1.0 / CAP)
+
+        def clip_scale(u):
+            c, b, heads = units[u]
+            rt[u] = new("rt_%d" % u, [P, PACK, len(heads) * QB], F32)
+            for r in range(PACK):
+                nc.vector.tensor_scalar(out=rt[u][:, r, :], in0=th[u][:, r, :], scalar1=0.0, scalar2=t4[:, c, r : r + 1],
+                                        op0=ALU.max, op1=ALU.mult)
+
+        def weigh(u):
+            c, b, heads = units[u]
+            w_bf[u] = new("w_bf_%d" % u, [P, len(heads) * QB, PACK], BF16)
+            nc.vector.tensor_tensor(
+                out=w_bf[u][:].rearrange("p (c i) r -> p c r i", i=4),
+                in0=rt[u][:].rearrange("p r (c i) -> p c r i", i=4),
+                in1=th[u][:].rearrange("p r (c i) -> p c r i", i=4),
+                op=ALU.mult,
+            )
+
+        def w_quantize(u):
+            c, b, heads = units[u]
+            w_codes[u] = new("w_codes_%d" % u, [P, len(heads) * QB], U32)
+            w_scales[u] = new("w_scales_%d" % u, [P, len(heads) * QB], U8)
+            quantize(w_codes[u][:], w_scales[u][:], w_bf[u][:].rearrange("p q r -> p (q r)"))
+            for x, h in enumerate(heads):
+                w_of[(c, b, h)] = (u, slice(x * QB, (x + 1) * QB))
+
+        den, rec = {}, {}
+
+        def values(u):
+            c, b, heads = units[u]
+            bank = y_banks[(u - 5) % 4]
+            for x, h in enumerate(heads):
+                for g in range(PASSES):
+                    wu, cols = w_of[(g, b, h)]
+                    e_cols = slice(h * E, (h + 1) * E)
+                    nc.tensor.matmul_mx(
+                        out=bank[:, x, :],
+                        lhsT=w_codes[wu][:, cols].bitcast(FP8X4), lhsT_scale=w_scales[wu][:, cols],
+                        rhs=v_codes[g][:, e_cols].bitcast(FP8X4), rhs_scale=v_scales[g][:, e_cols],
+                        start=(g == 0), stop=(g == PASSES - 1),
+                    )
+            den[u] = new("den_%d" % u, [P, len(heads)], F32)
+            nc.scalar.activation(out=den[u][:], in_=bank[:, : len(heads), E - 1], func=ACT.Identity, bias=1.0)
+
+        def invert(u):
+            c, b, heads = units[u]
+            rec[u] = new("rec_%d" % u, [P, len(heads)], F32)
+            nc.vector.reciprocal(out=rec[u][:], in_=den[u][:])
+
+        def finish(u):
+            c, b, heads = units[u]
+            bank = y_banks[(u - 5) % 4]
+            res = new("res_%d" % u, [P, len(heads), E], F32)
+            for x, h in enumerate(heads):
+                nc.scalar.activation(out=res[:, x, :], in_=bank[:, x, :], func=ACT.Copy, scale=rec[u][:, x : x + 1])
+            nc.sync.dma_start(out=out_rows[b][:, heads[0] : heads[-1] + 1, :], in_=res[:])
+
+        k_round(nc.vector.tensor_copy, 0, 0, k0_raw[0][:])
+        nc.vector.tensor_scalar(out=t4[:], in0=t_raw[:], scalar1=CAP * CAP, scalar2=None, op0=ALU.mult)
+        k_quantize_half(0, 0)
+        k_round(nc.vector.tensor_copy, 0, 1, k0_raw[1][:])
+        q_round(0)
+        k_quantize_half(0, 1)
+        q_quantize(0)
+        scores(0)
+        scores(1)
+        q_round(1)
+        q_quantize(1)
+        scores(2)
+        clip_scale(0)
+        q_round(2)
+
+        def k1_round(i):
+            k_round(nc.scalar.copy, 1, i, k1_raw[:, :, i * half : (i + 1) * half])
+
+        def k1_quantize():
+            quantize(k_codes[1][:], k_scales[1][:], k_bf[1][:].rearrange("p r s j -> p (r s j)"))
+
+        side = {
+            0: [lambda: q_quantize(2), lambda: k1_round(0), lambda: scores(3), lambda: k1_round(1), lambda: scores(4)],
+            2: [k1_quantize, lambda: scores(5), lambda: v_round(0), lambda: v_round(1)],
+            3: [lambda: scores(6)],
+            4: [lambda: v_quantize(0), lambda: scores(7)],
+            5: [lambda: v_quantize(1), lambda: scores(8), lambda: scores(9)],
+            6: [lambda: values(5)],
+            7: [lambda: invert(5), lambda: finish(5), lambda: values(6)],
+            8: [lambda: invert(6), lambda: finish(6), lambda: values(7)],
+            9: [lambda: invert(7), lambda: finish(7), lambda: values(8)],
+        }
+        for u in range(len(units)):
+            weigh(u)
+            if u + 1 < len(units):
+                clip_scale(u + 1)
+            for job in side.get(u, []):
+                job()
+            w_quantize(u)
+        invert(8)
+        finish(8)
+        values(9)
+        invert(9)
+        finish(9)

@@ -20,6 +20,7 @@ PASS = P * PACK
 PASSES = N // PASS
 QB = 128
 CAP = 2.0
+RUN = 2
 
 
 def tile_rows_a_relu2_cap_kernel(tc, qT, kT, t, v, out):
@@ -38,8 +39,8 @@ def tile_rows_a_relu2_cap_kernel(tc, qT, kT, t, v, out):
         def new(name, shape, dtype):
             return sb.tile(shape, dtype, name=name, align_bytes=64)
 
-        score_banks = [[ps.tile([P, PACK, QB], F32, name="score_%d_%d" % (h, i)) for i in range(2)] for h in range(H)]
-        y_banks = [ps.tile([P, H, E], F32, name="y_%d" % i) for i in range(4)]
+        score_banks = [[ps.tile([P, PASS], F32, name="score_%d_%d" % (h, i)) for i in range(2)] for h in range(H)]
+        y_banks = [ps.tile([P, 4, E], F32, name="y_%d" % i) for i in range(4)]
 
         t_raw = new("t_raw", [P, PASSES, PACK], F32)
         nc.scalar.dma_start(out=t_raw[:], in_=t_rows)
@@ -50,9 +51,18 @@ def tile_rows_a_relu2_cap_kernel(tc, qT, kT, t, v, out):
             return raw
 
         half = PASS // 2
-        k0_raw = [load("k0_raw_%d" % i, k_rows[:, :, i * half : (i + 1) * half], [P, PACK, half]) for i in range(2)]
         q_spans = [(0, 128), (128, 256), (256, 512)]
-        q_raw = [load("q_raw_%d" % a, q_rows[:, :, a:b], [P, PACK, b - a]) for a, b in q_spans]
+
+        def q_load(n):
+            a, b = q_spans[n]
+            return load("q_raw_%d" % n, q_rows[:, :, a:b], [P, PACK, b - a])
+
+        def k0_load(i):
+            return load("k0_raw_%d" % i, k_rows[:, :, i * half : (i + 1) * half], [P, PACK, half])
+
+        q_raw = [q_load(0)]
+        k0_raw = [k0_load(0), k0_load(1)]
+        q_raw.extend([q_load(1), q_load(2)])
         k1_raw = load("k1_raw", k_rows[:, :, PASS:], [P, PACK, PASS])
         v_raw = [load("v_raw_%d" % c, v_rows[c], [P, H, PACK * E]) for c in range(PASSES)]
 
@@ -63,10 +73,10 @@ def tile_rows_a_relu2_cap_kernel(tc, qT, kT, t, v, out):
         k_codes = [new("k_codes_%d" % c, [P, PASS], U32) for c in range(PASSES)]
         k_scales = [new("k_scales_%d" % c, [P, PASS], U8) for c in range(PASSES)]
 
-        def k_round(copy, c, i, raw):
+        def k_round(copy, c, s0, s1, raw, base):
             copy(
-                out=k_bf[c][:, :, i * 64 : (i + 1) * 64, :].rearrange("p r s j -> p s j r"),
-                in_=raw.rearrange("p j (s r) -> p s j r", r=PACK),
+                out=k_bf[c][:, :, s0:s1, :].rearrange("p r s j -> p s j r"),
+                in_=raw[:, :, (s0 - base) * PACK : (s1 - base) * PACK].rearrange("p j (s r) -> p s j r", r=PACK),
             )
 
         def k_quantize_half(c, i):
@@ -75,12 +85,19 @@ def tile_rows_a_relu2_cap_kernel(tc, qT, kT, t, v, out):
                 quantize(k_codes[c][:, cols], k_scales[c][:, cols],
                          k_bf[c][:, r, i * 64 : (i + 1) * 64, :].rearrange("p s j -> p (s j)"))
 
+        def k_quantize(c, r0=0, r1=PACK):
+            quantize(k_codes[c][:, r0 * P : r1 * P], k_scales[c][:, r0 * P : r1 * P],
+                     k_bf[c][:, r0:r1].rearrange("p r s j -> p (r s j)"))
+
+        def k1_round(s0, s1):
+            k_round(nc.scalar.copy, 1, s0, s1, k1_raw, 0)
+
         q_bf = [new("q_bf_%d" % a, [P, b - a, PACK], BF16) for a, b in q_spans]
         q_codes = [new("q_codes_%d" % a, [P, b - a], U32) for a, b in q_spans]
         q_scales = [new("q_scales_%d" % a, [P, b - a], U8) for a, b in q_spans]
 
-        def q_round(n):
-            nc.vector.tensor_copy(
+        def q_round(copy, n):
+            copy(
                 out=q_bf[n][:].rearrange("p (c i) j -> p c j i", i=4),
                 in_=q_raw[n][:].rearrange("p j (c i) -> p c j i", i=4),
             )
@@ -88,143 +105,222 @@ def tile_rows_a_relu2_cap_kernel(tc, qT, kT, t, v, out):
         def q_quantize(n):
             quantize(q_codes[n][:], q_scales[n][:], q_bf[n][:].rearrange("p q j -> p (q j)"))
 
-        v_bf = [new("v_bf_%d" % c, [P, H, E, PACK], BF16) for c in range(PASSES)]
-        v_codes = [new("v_codes_%d" % c, [P, H * E], U32) for c in range(PASSES)]
-        v_scales = [new("v_scales_%d" % c, [P, H * E], U8) for c in range(PASSES)]
+        v_bf = new("v_bf", [P, PASSES, H, E, PACK], BF16)
+        v_codes = new("v_codes", [P, PASSES, H * E], U32)
+        v_scales = new("v_scales", [P, PASSES, H * E], U8)
 
         def v_round(c):
             nc.scalar.copy(
-                out=v_bf[c][:].rearrange("p h (c i) j -> p h c j i", i=4),
+                out=v_bf[:, c].rearrange("p h (c i) j -> p h c j i", i=4),
                 in_=v_raw[c][:].rearrange("p h (j c i) -> p h c j i", j=PACK, i=4),
             )
 
-        def v_quantize(c):
-            quantize(v_codes[c][:], v_scales[c][:], v_bf[c][:].rearrange("p h e j -> p (h e j)"))
+        def v_quantize():
+            quantize(v_codes[:].rearrange("p c x -> p (c x)"), v_scales[:].rearrange("p c x -> p (c x)"),
+                     v_bf[:].rearrange("p c h e j -> p (c h e j)"))
 
         t4 = new("t4", [P, PASSES, PACK], F32)
 
-        units = [(0, 0, (0,)), (0, 0, (1,)), (0, 1, (0, 1)), (0, 2, (0, 1)), (0, 3, (0, 1)),
-                 (1, 0, (0, 1)), (1, 1, (0, 1)), (1, 2, (0, 1)), (1, 3, (0,)), (1, 3, (1,))]
-        th, rt, w_bf, w_codes, w_scales = {}, {}, {}, {}, {}
+        units = [(0, (0,), (0,)), (0, (0,), (1,)), (0, (1,), (0, 1)), (0, (2, 3), (0, 1)),
+                 (1, (0, 1), (0, 1)), (1, (2,), (0, 1)), (1, (3,), (0,)), (1, (3,), (1,))]
+        on_scalar = (6, 7)
+        th, rt, w_bf = {}, {}, {}
         w_of = {}
         turn = [0, 0]
 
-        def scores(u):
-            c, b, heads = units[u]
-            n = min(b, 2)
-            q_cols = slice(b * QB - q_spans[n][0], (b + 1) * QB - q_spans[n][0])
-            th[u] = new("th_%d" % u, [P, PACK, len(heads) * QB], F32)
-            for x, h in enumerate(heads):
-                bank = score_banks[h][turn[h] % 2]
-                turn[h] = turn[h] + 1
-                rows = slice(h * ROWS, (h + 1) * ROWS)
-                for r in range(PACK):
-                    cols = slice(r * P, (r + 1) * P)
-                    nc.tensor.matmul_mx(
-                        out=bank[:, r, :],
-                        lhsT=k_codes[c][rows, cols].bitcast(FP8X4), lhsT_scale=k_scales[c][rows, cols],
-                        rhs=q_codes[n][rows, q_cols].bitcast(FP8X4), rhs_scale=q_scales[n][rows, q_cols],
-                        start=True, stop=True,
-                    )
-                nc.scalar.activation(out=th[u][:, :, x * QB : (x + 1) * QB], in_=bank[:], func=ACT.Tanh, scale=1.0 / CAP)
+        def q_window(b):
+            n = [a <= b * QB < z for a, z in q_spans].index(True)
+            return n, slice(b * QB - q_spans[n][0], (b + 1) * QB - q_spans[n][0])
 
-        def clip_scale(u):
-            c, b, heads = units[u]
-            rt[u] = new("rt_%d" % u, [P, PACK, len(heads) * QB], F32)
-            for r in range(PACK):
+        def scores(u, groups=None):
+            c, blocks, heads = units[u]
+            width = len(blocks) * QB
+            places = PACK // len(blocks)
+            if u in on_scalar:
+                th[u] = new("th_%d" % u, [P, len(heads) * width, PACK], F32)
+            elif u not in th:
+                th[u] = new("th_%d" % u, [P, PACK, len(heads) * width], F32)
+            for g in groups or range(len(blocks)):
+                for x, h in enumerate(heads):
+                    bank = score_banks[h][turn[h] % 2][:].rearrange("p (r q) -> p r q", r=places)
+                    turn[h] = turn[h] + 1
+                    rows = slice(h * ROWS, (h + 1) * ROWS)
+                    for r in range(places):
+                        cols = slice((g * places + r) * P, (g * places + r + 1) * P)
+                        for i, b in enumerate(blocks):
+                            n, q_cols = q_window(b)
+                            nc.tensor.matmul_mx(
+                                out=bank[:, r, i * QB : (i + 1) * QB],
+                                lhsT=k_codes[c][rows, cols].bitcast(FP8X4), lhsT_scale=k_scales[c][rows, cols],
+                                rhs=q_codes[n][rows, q_cols].bitcast(FP8X4), rhs_scale=q_scales[n][rows, q_cols],
+                                start=True, stop=True,
+                            )
+                    if u in on_scalar:
+                        nc.scalar.activation(out=th[u][:, x * width : (x + 1) * width, :], in_=bank.rearrange("p r q -> p q r"),
+                                             func=ACT.Tanh, scale=1.0 / CAP)
+                    else:
+                        nc.scalar.activation(out=th[u][:, g * places : (g + 1) * places, x * width : (x + 1) * width], in_=bank,
+                                             func=ACT.Tanh, scale=1.0 / CAP)
+
+        clipped = {}
+
+        def s_clip(u):
+            clipped[u] = new("clip_%d" % u, list(th[u].shape), F32)
+            nc.scalar.activation(out=clipped[u][:], in_=th[u][:], func=ACT.Relu)
+
+        def s_square(u):
+            rt[u] = new("rt_%d" % u, list(th[u].shape), F32)
+            nc.scalar.activation(out=rt[u][:], in_=clipped[u][:], func=ACT.Square, scale=CAP)
+
+        def clip_scale(u, places=range(PACK)):
+            c, blocks, heads = units[u]
+            if u in on_scalar:
+                return
+            if u not in rt:
+                rt[u] = new("rt_%d" % u, list(th[u].shape), F32)
+            for r in places:
                 nc.vector.tensor_scalar(out=rt[u][:, r, :], in0=th[u][:, r, :], scalar1=0.0, scalar2=t4[:, c, r : r + 1],
                                         op0=ALU.max, op1=ALU.mult)
 
         def weigh(u):
-            c, b, heads = units[u]
-            w_bf[u] = new("w_bf_%d" % u, [P, len(heads) * QB, PACK], BF16)
+            c, blocks, heads = units[u]
+            width = len(heads) * len(blocks) * QB
+            w_bf[u] = new("w_bf_%d" % u, [P, width, PACK], BF16)
+            if u in on_scalar:
+                nc.vector.tensor_tensor(out=w_bf[u][:], in0=rt[u][:],
+                                        in1=t_raw[:, c, :].unsqueeze(1).to_broadcast([P, width, PACK]), op=ALU.mult)
+                return
             nc.vector.tensor_tensor(
-                out=w_bf[u][:].rearrange("p (c i) r -> p c r i", i=4),
-                in0=rt[u][:].rearrange("p r (c i) -> p c r i", i=4),
-                in1=th[u][:].rearrange("p r (c i) -> p c r i", i=4),
+                out=w_bf[u][:].rearrange("p (c i) r -> p c r i", i=RUN),
+                in0=rt[u][:].rearrange("p r (c i) -> p c r i", i=RUN),
+                in1=th[u][:].rearrange("p r (c i) -> p c r i", i=RUN),
                 op=ALU.mult,
             )
 
         def w_quantize(u):
-            c, b, heads = units[u]
-            w_codes[u] = new("w_codes_%d" % u, [P, len(heads) * QB], U32)
-            w_scales[u] = new("w_scales_%d" % u, [P, len(heads) * QB], U8)
-            quantize(w_codes[u][:], w_scales[u][:], w_bf[u][:].rearrange("p q r -> p (q r)"))
+            c, blocks, heads = units[u]
+            width = len(heads) * len(blocks) * QB
+            codes = new("w_codes_%d" % u, [P, width], U32)
+            scales = new("w_scales_%d" % u, [P, width], U8)
+            quantize(codes[:], scales[:], w_bf[u][:].rearrange("p q r -> p (q r)"))
             for x, h in enumerate(heads):
-                w_of[(c, b, h)] = (u, slice(x * QB, (x + 1) * QB))
+                for i, b in enumerate(blocks):
+                    cols = slice((x * len(blocks) + i) * QB, (x * len(blocks) + i + 1) * QB)
+                    w_of[(c, b, h)] = (codes[:, cols], scales[:, cols])
 
+        jobs = [((0, 1), (0, 1)), ((2,), (0, 1)), ((3,), (0,)), ((3,), (1,))]
         den, rec = {}, {}
 
-        def values(u):
-            c, b, heads = units[u]
-            bank = y_banks[(u - 5) % 4]
-            for x, h in enumerate(heads):
-                for g in range(PASSES):
-                    wu, cols = w_of[(g, b, h)]
-                    e_cols = slice(h * E, (h + 1) * E)
-                    nc.tensor.matmul_mx(
-                        out=bank[:, x, :],
-                        lhsT=w_codes[wu][:, cols].bitcast(FP8X4), lhsT_scale=w_scales[wu][:, cols],
-                        rhs=v_codes[g][:, e_cols].bitcast(FP8X4), rhs_scale=v_scales[g][:, e_cols],
-                        start=(g == 0), stop=(g == PASSES - 1),
-                    )
-            den[u] = new("den_%d" % u, [P, len(heads)], F32)
-            nc.scalar.activation(out=den[u][:], in_=bank[:, : len(heads), E - 1], func=ACT.Identity, bias=1.0)
+        def values(n, c):
+            blocks, heads = jobs[n]
+            sums = [(b, h) for b in blocks for h in heads]
+            for x, (b, h) in enumerate(sums):
+                codes, scales = w_of[(c, b, h)]
+                e_cols = slice(h * E, (h + 1) * E)
+                nc.tensor.matmul_mx(
+                    out=y_banks[n][:, x, :],
+                    lhsT=codes.bitcast(FP8X4), lhsT_scale=scales,
+                    rhs=v_codes[:, c, e_cols].bitcast(FP8X4), rhs_scale=v_scales[:, c, e_cols],
+                    start=(c == 0 and x == 0), stop=(c == PASSES - 1 and x == len(sums) - 1),
+                )
 
-        def invert(u):
-            c, b, heads = units[u]
-            rec[u] = new("rec_%d" % u, [P, len(heads)], F32)
-            nc.vector.reciprocal(out=rec[u][:], in_=den[u][:])
+        def plus_one(n, on_vector=False):
+            blocks, heads = jobs[n]
+            count = len(blocks) * len(heads)
+            den[n] = new("den_%d" % n, [P, count], F32)
+            if on_vector:
+                nc.vector.tensor_scalar(out=den[n][:], in0=y_banks[n][:, :count, E - 1], scalar1=1.0, scalar2=None, op0=ALU.add)
+            else:
+                nc.scalar.activation(out=den[n][:], in_=y_banks[n][:, :count, E - 1], func=ACT.Identity, bias=1.0)
 
-        def finish(u):
-            c, b, heads = units[u]
-            bank = y_banks[(u - 5) % 4]
-            res = new("res_%d" % u, [P, len(heads), E], F32)
-            for x, h in enumerate(heads):
-                nc.scalar.activation(out=res[:, x, :], in_=bank[:, x, :], func=ACT.Copy, scale=rec[u][:, x : x + 1])
-            nc.sync.dma_start(out=out_rows[b][:, heads[0] : heads[-1] + 1, :], in_=res[:])
+        def invert(n):
+            rec[n] = new("rec_%d" % n, list(den[n].shape), F32)
+            nc.vector.reciprocal(out=rec[n][:], in_=den[n][:])
 
-        k_round(nc.vector.tensor_copy, 0, 0, k0_raw[0][:])
+        def finish(n, on_vector=False):
+            blocks, heads = jobs[n]
+            for i, b in enumerate(blocks):
+                res = new("res_%d_%d" % (n, i), [P, len(heads), E], F32)
+                for j in range(len(heads)):
+                    x = i * len(heads) + j
+                    if on_vector:
+                        nc.vector.tensor_scalar(out=res[:, j, :], in0=y_banks[n][:, x, :], scalar1=rec[n][:, x : x + 1], scalar2=None, op0=ALU.mult)
+                    else:
+                        nc.scalar.activation(out=res[:, j, :], in_=y_banks[n][:, x, :], func=ACT.Copy, scale=rec[n][:, x : x + 1])
+                nc.sync.dma_start(out=out_rows[b][:, heads[0] : heads[-1] + 1, :], in_=res[:])
+
+        V, S = nc.vector.tensor_copy, nc.scalar.copy
+        q_round(V, 0)
         nc.vector.tensor_scalar(out=t4[:], in0=t_raw[:], scalar1=CAP * CAP, scalar2=None, op0=ALU.mult)
-        k_quantize_half(0, 0)
-        k_round(nc.vector.tensor_copy, 0, 1, k0_raw[1][:])
-        q_round(0)
-        k_quantize_half(0, 1)
         q_quantize(0)
+        k_round(V, 0, 0, 64, k0_raw[0], 0)
+        k_quantize_half(0, 0)
+        k_round(S, 0, 64, 96, k0_raw[1], 64)
+        k_round(V, 0, 96, 128, k0_raw[1], 64)
+        q_round(S, 1)
+        k_quantize_half(0, 1)
         scores(0)
         scores(1)
-        q_round(1)
         q_quantize(1)
         scores(2)
+        q_round(V, 2)
         clip_scale(0)
-        q_round(2)
-
-        def k1_round(i):
-            k_round(nc.scalar.copy, 1, i, k1_raw[:, :, i * half : (i + 1) * half])
-
-        def k1_quantize():
-            quantize(k_codes[1][:], k_scales[1][:], k_bf[1][:].rearrange("p r s j -> p (r s j)"))
-
-        side = {
-            0: [lambda: q_quantize(2), lambda: k1_round(0), lambda: scores(3), lambda: k1_round(1), lambda: scores(4)],
-            2: [k1_quantize, lambda: scores(5), lambda: v_round(0), lambda: v_round(1)],
-            3: [lambda: scores(6)],
-            4: [lambda: v_quantize(0), lambda: scores(7)],
-            5: [lambda: v_quantize(1), lambda: scores(8), lambda: scores(9)],
-            6: [lambda: values(5)],
-            7: [lambda: invert(5), lambda: finish(5), lambda: values(6)],
-            8: [lambda: invert(6), lambda: finish(6), lambda: values(7)],
-            9: [lambda: invert(7), lambda: finish(7), lambda: values(8)],
-        }
-        for u in range(len(units)):
-            weigh(u)
-            if u + 1 < len(units):
-                clip_scale(u + 1)
-            for job in side.get(u, []):
-                job()
-            w_quantize(u)
-        invert(8)
-        finish(8)
-        values(9)
-        invert(9)
-        finish(9)
+        q_quantize(2)
+        k1_round(0, 64)
+        scores(3, [0])
+        k1_round(64, 128)
+        scores(3, [1])
+        v_round(0)
+        weigh(0)
+        clip_scale(1)
+        w_quantize(0)
+        weigh(1)
+        clip_scale(2)
+        w_quantize(1)
+        weigh(2)
+        clip_scale(3, [0, 1])
+        k_quantize(1)
+        clip_scale(3, [2, 3])
+        scores(4)
+        v_round(1)
+        scores(5)
+        scores(6)
+        scores(7)
+        s_clip(6)
+        s_clip(7)
+        s_square(6)
+        s_square(7)
+        w_quantize(2)
+        weigh(3)
+        clip_scale(4)
+        w_quantize(3)
+        v_quantize()
+        values(0, 0)
+        values(1, 0)
+        values(2, 0)
+        values(3, 0)
+        weigh(4)
+        clip_scale(5)
+        w_quantize(4)
+        values(0, 1)
+        plus_one(0)
+        weigh(5)
+        weigh(6)
+        invert(0)
+        finish(0)
+        w_quantize(5)
+        values(1, 1)
+        plus_one(1)
+        weigh(7)
+        w_quantize(6)
+        values(2, 1)
+        plus_one(2)
+        invert(1)
+        w_quantize(7)
+        values(3, 1)
+        finish(1)
+        invert(2)
+        plus_one(3, True)
+        finish(2)
+        invert(3)
+        finish(3, True)

@@ -61,7 +61,7 @@ def tile_rows_a_relu2_cap_kernel(tc, qT, kT, t, v, out):
             return load("k0_raw_%d" % i, k_rows[:, :, i * half : (i + 1) * half], [P, PACK, half])
 
         q_raw = [q_load(0)]
-        k0_raw = [k0_load(0), k0_load(1)]
+        k0_raw = load("k0_raw", k_rows[:, :, :PASS], [P, PACK, PASS])
         q_raw.extend([q_load(1), q_load(2)])
         k1_raw = load("k1_raw", k_rows[:, :, PASS:], [P, PACK, PASS])
         v_raw = [load("v_raw_%d" % c, v_rows[c], [P, H, PACK * E]) for c in range(PASSES)]
@@ -96,23 +96,23 @@ def tile_rows_a_relu2_cap_kernel(tc, qT, kT, t, v, out):
         q_codes = [new("q_codes_%d" % a, [P, b - a], U32) for a, b in q_spans]
         q_scales = [new("q_scales_%d" % a, [P, b - a], U8) for a, b in q_spans]
 
-        def q_round(copy, n):
+        def q_round(copy, n, a=0, b=None):
             copy(
-                out=q_bf[n][:].rearrange("p (c i) j -> p c j i", i=4),
-                in_=q_raw[n][:].rearrange("p j (c i) -> p c j i", i=4),
+                out=q_bf[n][:, a:b, :].rearrange("p (c i) j -> p c j i", i=4),
+                in_=q_raw[n][:, :, a:b].rearrange("p j (c i) -> p c j i", i=4),
             )
 
-        def q_quantize(n):
-            quantize(q_codes[n][:], q_scales[n][:], q_bf[n][:].rearrange("p q j -> p (q j)"))
+        def q_quantize(n, a=0, b=None):
+            quantize(q_codes[n][:, a:b], q_scales[n][:, a:b], q_bf[n][:, a:b, :].rearrange("p q j -> p (q j)"))
 
         v_bf = new("v_bf", [P, PASSES, H, E, PACK], BF16)
         v_codes = new("v_codes", [P, PASSES, H * E], U32)
         v_scales = new("v_scales", [P, PASSES, H * E], U8)
 
-        def v_round(c):
+        def v_round(c, h0=0, h1=H):
             nc.scalar.copy(
-                out=v_bf[:, c].rearrange("p h (c i) j -> p h c j i", i=4),
-                in_=v_raw[c][:].rearrange("p h (j c i) -> p h c j i", j=PACK, i=4),
+                out=v_bf[:, c, h0:h1].rearrange("p h (c i) j -> p h c j i", i=4),
+                in_=v_raw[c][:, h0:h1].rearrange("p h (j c i) -> p h c j i", j=PACK, i=4),
             )
 
         def v_quantize():
@@ -132,18 +132,21 @@ def tile_rows_a_relu2_cap_kernel(tc, qT, kT, t, v, out):
             n = [a <= b * QB < z for a, z in q_spans].index(True)
             return n, slice(b * QB - q_spans[n][0], (b + 1) * QB - q_spans[n][0])
 
-        def scores(u, groups=None):
-            c, blocks, heads = units[u]
-            width = len(blocks) * QB
-            places = PACK // len(blocks)
-            if u in on_scalar:
-                th[u] = new("th_%d" % u, [P, len(heads) * width, PACK], F32)
-            elif u not in th:
-                th[u] = new("th_%d" % u, [P, PACK, len(heads) * width], F32)
-            for g in groups or range(len(blocks)):
-                for x, h in enumerate(heads):
-                    bank = score_banks[h][turn[h] % 2][:].rearrange("p (r q) -> p r q", r=places)
-                    turn[h] = turn[h] + 1
+        def scores(us, groups=None):
+            for g in groups or range(len(units[us[0]][1])):
+                fills = []
+                for u in us:
+                    c, blocks, heads = units[u]
+                    width = len(blocks) * QB
+                    places = PACK // len(blocks)
+                    if u not in th:
+                        shape = [P, len(heads) * width, PACK] if u in on_scalar else [P, PACK, len(heads) * width]
+                        th[u] = new("th_%d" % u, shape, F32)
+                    for x, h in enumerate(heads):
+                        bank = score_banks[h][turn[h] % 2][:].rearrange("p (r q) -> p r q", r=places)
+                        turn[h] = turn[h] + 1
+                        fills.append((u, x, h, bank))
+                for u, x, h, bank in fills:
                     rows = slice(h * ROWS, (h + 1) * ROWS)
                     for r in range(places):
                         cols = slice((g * places + r) * P, (g * places + r + 1) * P)
@@ -161,6 +164,12 @@ def tile_rows_a_relu2_cap_kernel(tc, qT, kT, t, v, out):
                     else:
                         nc.scalar.activation(out=th[u][:, g * places : (g + 1) * places, x * width : (x + 1) * width], in_=bank,
                                              func=ACT.Tanh, scale=1.0 / CAP)
+
+        def k_round_places(copy, c, raw, r0, r1, s0=0, s1=P):
+            copy(
+                out=k_bf[c][:, r0:r1, s0:s1, :].rearrange("p r s j -> p s j r"),
+                in_=raw[:].rearrange("p j (s r) -> p s j r", r=PACK)[:, s0:s1, :, r0:r1],
+            )
 
         clipped = {}
 
@@ -182,18 +191,19 @@ def tile_rows_a_relu2_cap_kernel(tc, qT, kT, t, v, out):
                 nc.vector.tensor_scalar(out=rt[u][:, r, :], in0=th[u][:, r, :], scalar1=0.0, scalar2=t4[:, c, r : r + 1],
                                         op0=ALU.max, op1=ALU.mult)
 
-        def weigh(u):
+        def weigh(u, a=0, b=None):
             c, blocks, heads = units[u]
             width = len(heads) * len(blocks) * QB
-            w_bf[u] = new("w_bf_%d" % u, [P, width, PACK], BF16)
+            if u not in w_bf:
+                w_bf[u] = new("w_bf_%d" % u, [P, width, PACK], BF16)
             if u in on_scalar:
                 nc.vector.tensor_tensor(out=w_bf[u][:], in0=rt[u][:],
                                         in1=t_raw[:, c, :].unsqueeze(1).to_broadcast([P, width, PACK]), op=ALU.mult)
                 return
             nc.vector.tensor_tensor(
-                out=w_bf[u][:].rearrange("p (c i) r -> p c r i", i=RUN),
-                in0=rt[u][:].rearrange("p r (c i) -> p c r i", i=RUN),
-                in1=th[u][:].rearrange("p r (c i) -> p c r i", i=RUN),
+                out=w_bf[u][:, a:b, :].rearrange("p (c i) r -> p c r i", i=RUN),
+                in0=rt[u][:, :, a:b].rearrange("p r (c i) -> p c r i", i=RUN),
+                in1=th[u][:, :, a:b].rearrange("p r (c i) -> p c r i", i=RUN),
                 op=ALU.mult,
             )
 
@@ -253,24 +263,22 @@ def tile_rows_a_relu2_cap_kernel(tc, qT, kT, t, v, out):
         q_round(V, 0)
         nc.vector.tensor_scalar(out=t4[:], in0=t_raw[:], scalar1=CAP * CAP, scalar2=None, op0=ALU.mult)
         q_quantize(0)
-        k_round(V, 0, 0, 64, k0_raw[0], 0)
-        k_quantize_half(0, 0)
-        k_round(S, 0, 64, 96, k0_raw[1], 64)
-        k_round(V, 0, 96, 128, k0_raw[1], 64)
+        k_round_places(V, 0, k0_raw, 0, 2)
+        k_round_places(S, 0, k0_raw, 2, 4, 0, 64)
+        k_round_places(V, 0, k0_raw, 2, 4, 64, 128)
+        k_quantize(0, 0, 2)
+        k_quantize(0, 2, 4)
         q_round(S, 1)
-        k_quantize_half(0, 1)
-        scores(0)
-        scores(1)
+        scores([0])
+        scores([1])
         q_quantize(1)
-        scores(2)
+        scores([2])
         q_round(V, 2)
         clip_scale(0)
         q_quantize(2)
-        k1_round(0, 64)
-        scores(3, [0])
-        k1_round(64, 128)
-        scores(3, [1])
-        v_round(0)
+        scores([3])
+        k_round_places(S, 1, k1_raw, 0, 2)
+        k_round_places(S, 1, k1_raw, 2, 4)
         weigh(0)
         clip_scale(1)
         w_quantize(0)
@@ -278,28 +286,29 @@ def tile_rows_a_relu2_cap_kernel(tc, qT, kT, t, v, out):
         clip_scale(2)
         w_quantize(1)
         weigh(2)
-        clip_scale(3, [0, 1])
-        k_quantize(1)
-        clip_scale(3, [2, 3])
-        scores(4)
+        clip_scale(3)
+        k_quantize(1, 0, 2)
+        scores([4], [0])
+        w_quantize(2)
+        k_quantize(1, 2, 4)
+        scores([4], [1])
+        weigh(3)
+        v_round(0)
         v_round(1)
-        scores(5)
-        scores(6)
-        scores(7)
+        scores([5])
+        scores([6, 7])
         s_clip(6)
         s_clip(7)
         s_square(6)
         s_square(7)
-        w_quantize(2)
-        weigh(3)
         clip_scale(4)
         w_quantize(3)
+        weigh(4)
         v_quantize()
         values(0, 0)
         values(1, 0)
         values(2, 0)
         values(3, 0)
-        weigh(4)
         clip_scale(5)
         w_quantize(4)
         values(0, 1)

@@ -51,7 +51,7 @@ def tile_rows_a_relu2_cap_kernel(tc, qT, kT, t, v, out):
             return raw
 
         half = PASS // 2
-        q_spans = [(0, 128), (128, 256), (256, 512)]
+        q_spans = [(0, 128), (128, 384), (384, 512)]
 
         def q_load(n):
             a, b = q_spans[n]
@@ -60,9 +60,8 @@ def tile_rows_a_relu2_cap_kernel(tc, qT, kT, t, v, out):
         def k0_load(i):
             return load("k0_raw_%d" % i, k_rows[:, :, i * half : (i + 1) * half], [P, PACK, half])
 
-        q_raw = [q_load(0)]
         k0_raw = load("k0_raw", k_rows[:, :, :PASS], [P, PACK, PASS])
-        q_raw.extend([q_load(1), q_load(2)])
+        q_raw = [q_load(n) for n in range(len(q_spans))]
         k1_raw = load("k1_raw", k_rows[:, :, PASS:], [P, PACK, PASS])
         v_raw = [load("v_raw_%d" % c, v_rows[c], [P, H, PACK * E]) for c in range(PASSES)]
 
@@ -146,18 +145,19 @@ def tile_rows_a_relu2_cap_kernel(tc, qT, kT, t, v, out):
                         bank = score_banks[h][turn[h] % 2][:].rearrange("p (r q) -> p r q", r=places)
                         turn[h] = turn[h] + 1
                         fills.append((u, x, h, bank))
-                for u, x, h, bank in fills:
-                    rows = slice(h * ROWS, (h + 1) * ROWS)
-                    for r in range(places):
-                        cols = slice((g * places + r) * P, (g * places + r + 1) * P)
-                        for i, b in enumerate(blocks):
-                            n, q_cols = q_window(b)
+                for r in range(places):
+                    cols = slice((g * places + r) * P, (g * places + r + 1) * P)
+                    for i, b in enumerate(blocks):
+                        n, q_cols = q_window(b)
+                        for u, x, h, bank in fills:
+                            rows = slice(h * ROWS, (h + 1) * ROWS)
                             nc.tensor.matmul_mx(
                                 out=bank[:, r, i * QB : (i + 1) * QB],
                                 lhsT=k_codes[c][rows, cols].bitcast(FP8X4), lhsT_scale=k_scales[c][rows, cols],
                                 rhs=q_codes[n][rows, q_cols].bitcast(FP8X4), rhs_scale=q_scales[n][rows, q_cols],
                                 start=True, stop=True,
                             )
+                for u, x, h, bank in fills:
                     if u in on_scalar:
                         nc.scalar.activation(out=th[u][:, x * width : (x + 1) * width, :], in_=bank.rearrange("p r q -> p q r"),
                                              func=ACT.Tanh, scale=1.0 / CAP)
@@ -260,25 +260,27 @@ def tile_rows_a_relu2_cap_kernel(tc, qT, kT, t, v, out):
                 nc.sync.dma_start(out=out_rows[b][:, heads[0] : heads[-1] + 1, :], in_=res[:])
 
         V, S = nc.vector.tensor_copy, nc.scalar.copy
-        q_round(V, 0)
-        nc.vector.tensor_scalar(out=t4[:], in0=t_raw[:], scalar1=CAP * CAP, scalar2=None, op0=ALU.mult)
-        q_quantize(0)
         k_round_places(V, 0, k0_raw, 0, 2)
         k_round_places(S, 0, k0_raw, 2, 4, 0, 64)
         k_round_places(V, 0, k0_raw, 2, 4, 64, 128)
-        k_quantize(0, 0, 2)
-        k_quantize(0, 2, 4)
-        q_round(S, 1)
+        q_round(S, 0)
+        k_quantize(0)
+        q_quantize(0)
+        q_round(V, 1, 0, 128)
+        nc.vector.tensor_scalar(out=t4[:], in0=t_raw[:], scalar1=CAP * CAP, scalar2=None, op0=ALU.mult)
+        q_round(S, 1, 128, 256)
         scores([0])
         scores([1])
-        q_quantize(1)
+        q_quantize(1, 0, 128)
         scores([2])
         q_round(V, 2)
+        q_quantize(1, 128, 256)
         clip_scale(0)
         q_quantize(2)
         scores([3])
         k_round_places(S, 1, k1_raw, 0, 2)
         k_round_places(S, 1, k1_raw, 2, 4)
+        v_round(0, 0, 1)
         weigh(0)
         clip_scale(1)
         w_quantize(0)
@@ -293,7 +295,7 @@ def tile_rows_a_relu2_cap_kernel(tc, qT, kT, t, v, out):
         k_quantize(1, 2, 4)
         scores([4], [1])
         weigh(3)
-        v_round(0)
+        v_round(0, 1, 2)
         v_round(1)
         scores([5])
         scores([6, 7])
@@ -312,24 +314,24 @@ def tile_rows_a_relu2_cap_kernel(tc, qT, kT, t, v, out):
         clip_scale(5)
         w_quantize(4)
         values(0, 1)
-        plus_one(0)
         weigh(5)
+        plus_one(0, True)
         weigh(6)
         invert(0)
         finish(0)
         w_quantize(5)
         values(1, 1)
-        plus_one(1)
         weigh(7)
         w_quantize(6)
         values(2, 1)
-        plus_one(2)
-        invert(1)
+        plus_one(1, True)
         w_quantize(7)
         values(3, 1)
+        invert(1)
         finish(1)
-        invert(2)
+        plus_one(2, True)
         plus_one(3, True)
-        finish(2)
+        invert(2)
         invert(3)
+        finish(2, True)
         finish(3, True)

from contextlib import ExitStack

import concourse.mybir as mybir

H, D, NQ, N, E = 2, 256, 512, 1024, 128
FLOPS = 2 * H * N * NQ * D + 2 * H * NQ * N * E

F32 = mybir.dt.float32
BF16 = mybir.dt.bfloat16
U32 = mybir.dt.uint32
U8 = mybir.dt.uint8
FP8X4 = mybir.dt.float8_e4m3fn_x4
ACT = mybir.ActivationFunctionType
ALU = mybir.AluOpType

P = 128
PACK = 4
ROWS = D // PACK
PASS = P * PACK
PASSES = N // PASS
QB = 128
CAP = 2.0
RUN = 2


def tile_rows_a_relu2_cap_kernel(tc, qT, kT, t, v, out):
    nc = tc.nc
    q_rows = qT.rearrange("h (p j) q -> (h p) j q", j=PACK)
    k_rows = kT.rearrange("h (p j) n -> (h p) j n", j=PACK)
    v_rows = v.rearrange("h (c p j) e -> c p h (j e)", p=P, j=PACK)
    t_rows = t.rearrange("(c p j) o -> p c (j o)", p=P, j=PACK)
    out_rows = out.rearrange("h (b m) e -> b m h e", m=QB)

    with ExitStack() as ctx:
        sb = ctx.enter_context(tc.tile_pool(name="sb", bufs=1))
        ps = ctx.enter_context(tc.psum_pool(name="ps", bufs=1))
        ctx.enter_context(tc.manual_schedule())

        def new(name, shape, dtype):
            return sb.tile(shape, dtype, name=name, align_bytes=64)

        score_banks = [[ps.tile([P, PASS], F32, name="score_%d_%d" % (h, i)) for i in range(2)] for h in range(H)]
        y_banks = [ps.tile([P, 4, E], F32, name="y_%d" % i) for i in range(4)]

        t_raw = new("t_raw", [P, PASSES, PACK], F32)
        nc.scalar.dma_start(out=t_raw[:], in_=t_rows)

        def load(name, src, shape):
            raw = new(name, shape, F32)
            nc.sync.dma_start(out=raw[:], in_=src)
            return raw

        half = PASS // 2
        q_spans = [(0, 128), (128, 384), (384, 512)]

        def q_load(n):
            a, b = q_spans[n]
            return load("q_raw_%d" % n, q_rows[:, :, a:b], [P, PACK, b - a])

        def k0_load(i):
            return load("k0_raw_%d" % i, k_rows[:, :, i * half : (i + 1) * half], [P, PACK, half])

        k0_raw = load("k0_raw", k_rows[:, :, :PASS], [P, PACK, PASS])
        q_raw = [q_load(n) for n in range(len(q_spans))]
        k1_raw = load("k1_raw", k_rows[:, :, PASS:], [P, PACK, PASS])
        v_raw = [load("v_raw_%d" % c, v_rows[c], [P, H, PACK * E]) for c in range(PASSES)]

        def quantize(codes, scales, src):
            nc.vector.quantize_mx(out=codes.bitcast(FP8X4), scales=scales, in_=src)

        k_bf = [new("k_bf_%d" % c, [P, PACK, P, PACK], BF16) for c in range(PASSES)]
        k_codes = [new("k_codes_%d" % c, [P, PASS], U32) for c in range(PASSES)]
        k_scales = [new("k_scales_%d" % c, [P, PASS], U8) for c in range(PASSES)]

        def k_round(copy, c, s0, s1, raw, base):
            copy(
                out=k_bf[c][:, :, s0:s1, :].rearrange("p r s j -> p s j r"),
                in_=raw[:, :, (s0 - base) * PACK : (s1 - base) * PACK].rearrange("p j (s r) -> p s j r", r=PACK),
            )

        def k_quantize_half(c, i):
            for r in range(PACK):
                cols = slice(r * P + i * 64, r * P + (i + 1) * 64)
                quantize(k_codes[c][:, cols], k_scales[c][:, cols],
                         k_bf[c][:, r, i * 64 : (i + 1) * 64, :].rearrange("p s j -> p (s j)"))

        def k_quantize(c, r0=0, r1=PACK):
            quantize(k_codes[c][:, r0 * P : r1 * P], k_scales[c][:, r0 * P : r1 * P],
                     k_bf[c][:, r0:r1].rearrange("p r s j -> p (r s j)"))

        def k1_round(s0, s1):
            k_round(nc.scalar.copy, 1, s0, s1, k1_raw, 0)

        q_bf = [new("q_bf_%d" % a, [P, b - a, PACK], BF16) for a, b in q_spans]
        q_codes = [new("q_codes_%d" % a, [P, b - a], U32) for a, b in q_spans]
        q_scales = [new("q_scales_%d" % a, [P, b - a], U8) for a, b in q_spans]

        def q_round(copy, n, a=0, b=None):
            copy(
                out=q_bf[n][:, a:b, :].rearrange("p (c i) j -> p c j i", i=4),
                in_=q_raw[n][:, :, a:b].rearrange("p j (c i) -> p c j i", i=4),
            )

        def q_quantize(n, a=0, b=None):
            quantize(q_codes[n][:, a:b], q_scales[n][:, a:b], q_bf[n][:, a:b, :].rearrange("p q j -> p (q j)"))

        v_bf = new("v_bf", [P, PASSES, H, E, PACK], BF16)
        v_codes = new("v_codes", [P, PASSES, H * E], U32)
        v_scales = new("v_scales", [P, PASSES, H * E], U8)

        def v_round(c, h0=0, h1=H):
            nc.scalar.copy(
                out=v_bf[:, c, h0:h1].rearrange("p h (c i) j -> p h c j i", i=4),
                in_=v_raw[c][:, h0:h1].rearrange("p h (j c i) -> p h c j i", j=PACK, i=4),
            )

        def v_quantize():
            quantize(v_codes[:].rearrange("p c x -> p (c x)"), v_scales[:].rearrange("p c x -> p (c x)"),
                     v_bf[:].rearrange("p c h e j -> p (c h e j)"))

        t4 = new("t4", [P, PASSES, PACK], F32)

        units = [(0, (0,), (0,)), (0, (0,), (1,)), (0, (1,), (0, 1)), (0, (2, 3), (0, 1)),
                 (1, (0, 1), (0, 1)), (1, (2,), (0, 1)), (1, (3,), (0,)), (1, (3,), (1,))]
        on_scalar = (6, 7)
        th, rt, w_bf = {}, {}, {}
        w_of = {}
        turn = [0, 0]

        def q_window(b):
            n = [a <= b * QB < z for a, z in q_spans].index(True)
            return n, slice(b * QB - q_spans[n][0], (b + 1) * QB - q_spans[n][0])

        def scores(us, groups=None):
            for g in groups or range(len(units[us[0]][1])):
                fills = []
                for u in us:
                    c, blocks, heads = units[u]
                    width = len(blocks) * QB
                    places = PACK // len(blocks)
                    if u not in th:
                        shape = [P, len(heads) * width, PACK] if u in on_scalar else [P, PACK, len(heads) * width]
                        th[u] = new("th_%d" % u, shape, F32)
                    for x, h in enumerate(heads):
                        bank = score_banks[h][turn[h] % 2][:].rearrange("p (r q) -> p r q", r=places)
                        turn[h] = turn[h] + 1
                        fills.append((u, x, h, bank))
                for r in range(places):
                    cols = slice((g * places + r) * P, (g * places + r + 1) * P)
                    for i, b in enumerate(blocks):
                        n, q_cols = q_window(b)
                        for u, x, h, bank in fills:
                            rows = slice(h * ROWS, (h + 1) * ROWS)
                            nc.tensor.matmul_mx(
                                out=bank[:, r, i * QB : (i + 1) * QB],
                                lhsT=k_codes[c][rows, cols].bitcast(FP8X4), lhsT_scale=k_scales[c][rows, cols],
                                rhs=q_codes[n][rows, q_cols].bitcast(FP8X4), rhs_scale=q_scales[n][rows, q_cols],
                                start=True, stop=True,
                            )
                for u, x, h, bank in fills:
                    if u in on_scalar:
                        nc.scalar.activation(out=th[u][:, x * width : (x + 1) * width, :], in_=bank.rearrange("p r q -> p q r"),
                                             func=ACT.Tanh, scale=1.0 / CAP)
                    else:
                        nc.scalar.activation(out=th[u][:, g * places : (g + 1) * places, x * width : (x + 1) * width], in_=bank,
                                             func=ACT.Tanh, scale=1.0 / CAP)

        def k_round_places(copy, c, raw, r0, r1, s0=0, s1=P):
            copy(
                out=k_bf[c][:, r0:r1, s0:s1, :].rearrange("p r s j -> p s j r"),
                in_=raw[:].rearrange("p j (s r) -> p s j r", r=PACK)[:, s0:s1, :, r0:r1],
            )

        clipped = {}

        def s_clip(u):
            clipped[u] = new("clip_%d" % u, list(th[u].shape), F32)
            nc.scalar.activation(out=clipped[u][:], in_=th[u][:], func=ACT.Relu)

        def s_square(u):
            rt[u] = new("rt_%d" % u, list(th[u].shape), F32)
            nc.scalar.activation(out=rt[u][:], in_=clipped[u][:], func=ACT.Square, scale=CAP)

        def clip_scale(u, places=range(PACK)):
            c, blocks, heads = units[u]
            if u in on_scalar:
                return
            if u not in rt:
                rt[u] = new("rt_%d" % u, list(th[u].shape), F32)
            for r in places:
                nc.vector.tensor_scalar(out=rt[u][:, r, :], in0=th[u][:, r, :], scalar1=0.0, scalar2=t4[:, c, r : r + 1],
                                        op0=ALU.max, op1=ALU.mult)

        def weigh(u, a=0, b=None):
            c, blocks, heads = units[u]
            width = len(heads) * len(blocks) * QB
            if u not in w_bf:
                w_bf[u] = new("w_bf_%d" % u, [P, width, PACK], BF16)
            if u in on_scalar:
                nc.vector.tensor_tensor(out=w_bf[u][:], in0=rt[u][:],
                                        in1=t_raw[:, c, :].unsqueeze(1).to_broadcast([P, width, PACK]), op=ALU.mult)
                return
            nc.vector.tensor_tensor(
                out=w_bf[u][:, a:b, :].rearrange("p (c i) r -> p c r i", i=RUN),
                in0=rt[u][:, :, a:b].rearrange("p r (c i) -> p c r i", i=RUN),
                in1=th[u][:, :, a:b].rearrange("p r (c i) -> p c r i", i=RUN),
                op=ALU.mult,
            )

        def w_quantize(u):
            c, blocks, heads = units[u]
            width = len(heads) * len(blocks) * QB
            codes = new("w_codes_%d" % u, [P, width], U32)
            scales = new("w_scales_%d" % u, [P, width], U8)
            quantize(codes[:], scales[:], w_bf[u][:].rearrange("p q r -> p (q r)"))
            for x, h in enumerate(heads):
                for i, b in enumerate(blocks):
                    cols = slice((x * len(blocks) + i) * QB, (x * len(blocks) + i + 1) * QB)
                    w_of[(c, b, h)] = (codes[:, cols], scales[:, cols])

        jobs = [((0, 1), (0, 1)), ((2,), (0, 1)), ((3,), (0,)), ((3,), (1,))]
        den, rec = {}, {}

        def values(n, c):
            blocks, heads = jobs[n]
            sums = [(b, h) for b in blocks for h in heads]
            for x, (b, h) in enumerate(sums):
                codes, scales = w_of[(c, b, h)]
                e_cols = slice(h * E, (h + 1) * E)
                nc.tensor.matmul_mx(
                    out=y_banks[n][:, x, :],
                    lhsT=codes.bitcast(FP8X4), lhsT_scale=scales,
                    rhs=v_codes[:, c, e_cols].bitcast(FP8X4), rhs_scale=v_scales[:, c, e_cols],
                    start=(c == 0 and x == 0), stop=(c == PASSES - 1 and x == len(sums) - 1),
                )

        def plus_one(n, on_vector=False):
            blocks, heads = jobs[n]
            count = len(blocks) * len(heads)
            den[n] = new("den_%d" % n, [P, count], F32)
            if on_vector:
                nc.vector.tensor_scalar(out=den[n][:], in0=y_banks[n][:, :count, E - 1], scalar1=1.0, scalar2=None, op0=ALU.add)
            else:
                nc.scalar.activation(out=den[n][:], in_=y_banks[n][:, :count, E - 1], func=ACT.Identity, bias=1.0)

        def invert(n):
            rec[n] = new("rec_%d" % n, list(den[n].shape), F32)
            nc.vector.reciprocal(out=rec[n][:], in_=den[n][:])

        def finish(n, on_vector=False):
            blocks, heads = jobs[n]
            for i, b in enumerate(blocks):
                res = new("res_%d_%d" % (n, i), [P, len(heads), E], F32)
                for j in range(len(heads)):
                    x = i * len(heads) + j
                    if on_vector:
                        nc.vector.tensor_scalar(out=res[:, j, :], in0=y_banks[n][:, x, :], scalar1=rec[n][:, x : x + 1], scalar2=None, op0=ALU.mult)
                    else:
                        nc.scalar.activation(out=res[:, j, :], in_=y_banks[n][:, x, :], func=ACT.Copy, scale=rec[n][:, x : x + 1])
                nc.sync.dma_start(out=out_rows[b][:, heads[0] : heads[-1] + 1, :], in_=res[:])

        V, S = nc.vector.tensor_copy, nc.scalar.copy
        k_round_places(V, 0, k0_raw, 0, 2)
        k_round_places(S, 0, k0_raw, 2, 4, 0, 64)
        k_round_places(V, 0, k0_raw, 2, 4, 64, 128)
        q_round(S, 0)
        k_quantize(0)
        q_quantize(0)
        q_round(V, 1, 0, 128)
        nc.vector.tensor_scalar(out=t4[:], in0=t_raw[:], scalar1=CAP * CAP, scalar2=None, op0=ALU.mult)
        q_round(S, 1, 128, 256)
        scores([0])
        scores([1])
        q_quantize(1, 0, 128)
        scores([2])
        q_round(V, 2)
        q_quantize(1, 128, 256)
        clip_scale(0)
        q_quantize(2)
        scores([3])
        k_round_places(S, 1, k1_raw, 0, 2)
        k_round_places(S, 1, k1_raw, 2, 4)
        v_round(0, 0, 1)
        weigh(0)
        clip_scale(1)
        w_quantize(0)
        weigh(1)
        clip_scale(2)
        w_quantize(1)
        weigh(2)
        clip_scale(3)
        k_quantize(1, 0, 2)
        scores([4], [0])
        w_quantize(2)
        k_quantize(1, 2, 4)
        scores([4], [1])
        weigh(3)
        v_round(0, 1, 2)
        v_round(1)
        scores([5])
        scores([6, 7])
        s_clip(6)
        s_clip(7)
        s_square(6)
        s_square(7)
        clip_scale(4)
        w_quantize(3)
        weigh(4)
        v_quantize()
        values(0, 0)
        values(1, 0)
        values(2, 0)
        values(3, 0)
        clip_scale(5)
        w_quantize(4)
        values(0, 1)
        weigh(5)
        plus_one(0, True)
        weigh(6)
        invert(0)
        finish(0)
        w_quantize(5)
        values(1, 1)
        weigh(7)
        w_quantize(6)
        values(2, 1)
        plus_one(1, True)
        w_quantize(7)
        values(3, 1)
        invert(1)
        finish(1)
        plus_one(2, True)
        plus_one(3, True)
        invert(2)
        invert(3)
        finish(2, True)
        finish(3, True)
